import numpy as np
CORES = [3,59,83]
N = 3
def setup_inputs(rng):
    return {"x": rng.standard_normal((N, 128, 12), dtype=np.float32)}
def reference(x):
    b = 12 // N
    blocks = x.reshape(N, 128, N, b)
    return {"y": np.ascontiguousarray(blocks.transpose(2, 1, 0, 3)).reshape(N, 128, 12)}

@@ -1,0 +1,38 @@
+import concourse.bass as bass
+
+SCRATCH = {
+    "stage": ("dram", [128, 12], "float32"),
+    "land": ("dram", [3, 128, 12], "float32"),
+}
+SEMAPHORES = ["loaded", "arrived", "stored"]
+
+B = 4
+
+
+def rank_program(g, core, T, topo):
+    r = T.rank_of(core)
+    if r is None:
+        return
+    peers = [j for j in range(len(T.cores)) if j != r]
+
+    g.dma_start(T.stage[:], T.x[:]).then_inc(T.sem.loaded, 16)
+    g.wait_ge(T.sem.loaded, 16)
+
+    transfers = []
+    for k, j in enumerate(peers):
+        rid, pid, _se = topo.addr(T.cores[j])
+        transfers.append(bass.RemoteDMATransfer(
+            dst_ids=[bass.DstId(rid=rid, pnc=pid)],
+            dma_engine_mask=0x0F << (4 * k),
+            remote_sem=T.sem.arrived,
+            src=T.stage[:],
+            dst=T.land[r],
+        ))
+    g.remote_dma_fused(transfers, local_sem=T.sem.arrived)
+
+    g.dma_start(T.y[:, B * r:B * r + B], T.x[:, B * r:B * r + B]).then_inc(T.sem.stored, 16)
+
+    g.wait_ge(T.sem.arrived, 16)
+    for j in peers:
+        g.dma_start(T.y[:, B * j:B * j + B], T.land[j, :, B * r:B * r + B]).then_inc(T.sem.stored, 16)
+    g.wait_ge(T.sem.stored, 48)

@@ -18,21 +18,21 @@ def rank_program(g, core, T, topo):
     g.dma_start(T.stage[:], T.x[:]).then_inc(T.sem.loaded, 16)
     g.wait_ge(T.sem.loaded, 16)
 
-    transfers = []
-    for k, j in enumerate(peers):
+    ids = []
+    for j in peers:
         rid, pid, _se = topo.addr(T.cores[j])
-        transfers.append(bass.RemoteDMATransfer(
-            dst_ids=[bass.DstId(rid=rid, pnc=pid)],
-            dma_engine_mask=0x0F << (4 * k),
-            remote_sem=T.sem.arrived,
-            src=T.stage[:],
-            dst=T.land[r],
-        ))
-    g.remote_dma_fused(transfers, local_sem=T.sem.arrived)
+        ids.append(bass.DstId(rid=rid, pnc=pid))
+    g.remote_dma_fused([bass.RemoteDMATransfer(
+        dst_ids=ids,
+        dma_engine_mask=0xFF,
+        remote_sem=T.sem.arrived,
+        srcs=[T.stage[:]],
+        dsts=[T.land[r] for _j in peers],
+    )], local_sem=T.sem.arrived)
 
     g.dma_start(T.y[:, B * r:B * r + B], T.x[:, B * r:B * r + B]).then_inc(T.sem.stored, 16)
 
-    g.wait_ge(T.sem.arrived, 16)
+    g.wait_ge(T.sem.arrived, 24)
     for j in peers:
         g.dma_start(T.y[:, B * j:B * j + B], T.land[j, :, B * r:B * r + B]).then_inc(T.sem.stored, 16)
     g.wait_ge(T.sem.stored, 48)

@@ -3,9 +3,9 @@ import concourse.bass as bass
 SCRATCH = {
     "stage": ("dram", [128, 12], "float32"),
     "land": ("dram", [3, 128, 12], "float32"),
+    "asm": ("sbuf", [128, 3, 12], "float32"),
 }
-SEMAPHORES = ["loaded", "arrived", "stored"]
-
+SEMAPHORES = ["loaded", "own", "from0", "from1", "from2", "sent", "stored"]
 B = 4
 
 
@@ -13,9 +13,13 @@ def rank_program(g, core, T, topo):
     r = T.rank_of(core)
     if r is None:
         return
-    peers = [j for j in range(len(T.cores)) if j != r]
+    frm = [T.sem.from0, T.sem.from1, T.sem.from2]
+    o = 1
+    peers = [j for j in range(3) if j != r]
 
     g.dma_start(T.stage[:], T.x[:]).then_inc(T.sem.loaded, 16)
+    if r == o:
+        g.dma_start(T.asm[:, r, B * r:B * r + B], T.x[:, B * r:B * r + B]).then_inc(T.sem.own, 16)
     g.wait_ge(T.sem.loaded, 16)
 
     ids = []
@@ -25,14 +29,23 @@ def rank_program(g, core, T, topo):
     g.remote_dma_fused([bass.RemoteDMATransfer(
         dst_ids=ids,
         dma_engine_mask=0xFF,
-        remote_sem=T.sem.arrived,
+        remote_sem=frm[r],
         srcs=[T.stage[:]],
-        dsts=[T.land[r] for _j in peers],
-    )], local_sem=T.sem.arrived)
+        dsts=[(T.asm[:, r, :] if j == o else T.land[r]) for j in peers],
+    )], local_sem=T.sem.sent)
 
-    g.dma_start(T.y[:, B * r:B * r + B], T.x[:, B * r:B * r + B]).then_inc(T.sem.stored, 16)
-
-    g.wait_ge(T.sem.arrived, 24)
-    for j in peers:
-        g.dma_start(T.y[:, B * j:B * j + B], T.land[j, :, B * r:B * r + B]).then_inc(T.sem.stored, 16)
-    g.wait_ge(T.sem.stored, 48)
+    if r == o:
+        g.wait_ge(T.sem.own, 16)
+        for j in peers:
+            g.wait_ge(frm[j], 8)
+        g.dma_start(T.y[:], T.asm[:, :, B * r:B * r + B]).then_inc(T.sem.stored, 16)
+        g.wait_ge(T.sem.sent, 8)
+        g.wait_ge(T.sem.stored, 16)
+    else:
+        n = 2 - r
+        g.dma_start(T.y[:, B * r:B * r + B], T.x[:, B * r:B * r + B]).then_inc(T.sem.stored, 16)
+        for j in (n, o):
+            g.wait_ge(frm[j], 8)
+            g.dma_start(T.y[:, B * j:B * j + B], T.land[j, :, B * r:B * r + B]).then_inc(T.sem.stored, 16)
+        g.wait_ge(T.sem.sent, 8)
+        g.wait_ge(T.sem.stored, 48)

import concourse.bass as bass

SCRATCH = {
    "stage": ("dram", [128, 12], "float32"),
    "land": ("dram", [3, 128, 12], "float32"),
    "asm": ("sbuf", [128, 3, 12], "float32"),
}
SEMAPHORES = ["loaded", "own", "from0", "from1", "from2", "sent", "stored"]
B = 4


def rank_program(g, core, T, topo):
    r = T.rank_of(core)
    if r is None:
        return
    frm = [T.sem.from0, T.sem.from1, T.sem.from2]
    o = 1
    peers = [j for j in range(3) if j != r]

    g.dma_start(T.stage[:], T.x[:]).then_inc(T.sem.loaded, 16)
    if r == o:
        g.dma_start(T.asm[:, r, B * r:B * r + B], T.x[:, B * r:B * r + B]).then_inc(T.sem.own, 16)
    g.wait_ge(T.sem.loaded, 16)

    ids = []
    for j in peers:
        rid, pid, _se = topo.addr(T.cores[j])
        ids.append(bass.DstId(rid=rid, pnc=pid))
    g.remote_dma_fused([bass.RemoteDMATransfer(
        dst_ids=ids,
        dma_engine_mask=0xFF,
        remote_sem=frm[r],
        srcs=[T.stage[:]],
        dsts=[(T.asm[:, r, :] if j == o else T.land[r]) for j in peers],
    )], local_sem=T.sem.sent)

    if r == o:
        g.wait_ge(T.sem.own, 16)
        for j in peers:
            g.wait_ge(frm[j], 8)
        g.dma_start(T.y[:], T.asm[:, :, B * r:B * r + B]).then_inc(T.sem.stored, 16)
        g.wait_ge(T.sem.sent, 8)
        g.wait_ge(T.sem.stored, 16)
    else:
        n = 2 - r
        g.dma_start(T.y[:, B * r:B * r + B], T.x[:, B * r:B * r + B]).then_inc(T.sem.stored, 16)
        for j in (n, o):
            g.wait_ge(frm[j], 8)
            g.dma_start(T.y[:, B * j:B * j + B], T.land[j, :, B * r:B * r + B]).then_inc(T.sem.stored, 16)
        g.wait_ge(T.sem.sent, 8)
        g.wait_ge(T.sem.stored, 48)
